import numpy as np
import ml_dtypes


def mxq(x, axis, fmt="e4m3"):
    dtype, down = {"e4m3": (ml_dtypes.float8_e4m3fn, 7), "e5m2": (ml_dtypes.float8_e5m2, 14)}[fmt]
    v = np.moveaxis(np.asarray(x, np.float32).astype(ml_dtypes.bfloat16).astype(np.float64), axis, -1)
    blocks = v.reshape(v.shape[:-1] + (-1, 32))
    amax = np.abs(blocks).max(-1, keepdims=True)
    byte = np.maximum(np.where(amax > 0, np.frexp(amax)[1] - 1 + 127, 0) - down, 1)
    scale = np.exp2(byte - 127.0)
    codes = (blocks / scale).astype(np.float32).astype(dtype).astype(np.float64)
    return np.moveaxis((codes * scale).reshape(v.shape), -1, axis)


WIDE = False


def mx_kscale(k):
    if not WIDE:
        return np.ones(k)
    levels = np.array([10, -10, 5, -5, 0])
    if k % 512:
        return np.exp2(np.random.permutation(np.resize(levels, k // 32))).repeat(32)
    a = np.empty((k // 512, 16))
    for p in range(k // 512):
        a[p, :8] = np.random.permutation(np.resize(levels, 8))
        for g in range(8):
            far = levels[np.abs(levels - a[p, g]) >= 10]
            a[p, g + 8] = far[np.random.randint(len(far))]
    return np.exp2(a.ravel()).repeat(32)


def f64(x):
    return np.asarray(x).astype(np.float64)


def striped(idx):
    return np.tile(idx.reshape(-1, 16).T, (8, 1)).astype(np.uint16)


def unstriped(offs):
    return offs[:16].T.reshape(-1).astype(np.int64)


def striped8(idx):
    return np.concatenate([x.reshape(-1, 16).T for x in idx]).astype(np.uint16)


def runs(offs, k):
    lists = np.stack([offs[16 * r : 16 * r + 16].T.reshape(-1) for r in range(8)]).astype(np.int64)
    return lists[np.arange(k) % 512 // 64]


def pack_weight(w):
    k, n = w.shape
    w = f64(np.asarray(w, np.float32).astype(ml_dtypes.bfloat16)).reshape(k // 32, 32, n)
    amax = np.abs(w).max(1)
    byte = np.clip(np.where(amax > 0, np.frexp(amax)[1] - 1 + 127 - 7, 1), 1, 254)
    scaled = (w * np.exp2(127.0 - byte)[:, None, :]).reshape(k, n).astype(np.float32)
    words = np.ascontiguousarray(scaled.reshape(k // 512, 128, 4, n).transpose(0, 1, 3, 2)).astype(ml_dtypes.float8_e4m3fn).view(np.uint8)
    return words, np.ascontiguousarray(byte.astype(np.uint8).reshape(k // 512, 16, n))


def unpack_weight(words, scales):
    g, p, n, _ = words.shape
    vals = np.ascontiguousarray(words).view(ml_dtypes.float8_e4m3fn).astype(np.float64) * np.repeat(np.exp2(scales.astype(np.float64) - 127.0), 8, axis=1)[..., None]
    return vals.transpose(0, 1, 3, 2).reshape(g * 512, n)


K, T, S, N, G, H = 512, 2048, 256, 512, 2048, 512


def setup_inputs():
    n = np.random.standard_normal
    s = mx_kscale(K)[:, None]
    u = mx_kscale(K)
    packed_xT = pack_weight(n((K, T)) * s)
    packed_dT = pack_weight(n((K, G)) / s)
    return {
        "x_words": packed_xT[0],
        "x_scales": packed_xT[1],
        "d_words": packed_dT[0],
        "d_scales": packed_dT[1],
        "gn": (np.random.uniform(0.5, 1.5, (H, 1)) * u[:, None]).astype(np.float32),
        "w1": (n((H, N)) / np.sqrt(2 * H) / u[:, None]).astype(np.float32),
        "w2": (n((K, N)) / np.sqrt(2 * K) / s).astype(np.float32),
        "tau": np.random.uniform(0.5, 1.2, (N, 1)).astype(np.float32),
        "offs": striped(np.random.permutation(T)[:S]),
        "k1": striped8(np.random.randint(0, G, (8, H))),
        "n1": striped(np.random.permutation(S)),
        "n2": striped(np.random.permutation(S)),
        "two": striped(np.random.permutation(T)[:S]),
        "n3": striped(np.random.permutation(S)),
        "n4": striped(np.random.permutation(S)),
    }


def reference(x_words, x_scales, d_words, d_scales, gn, w1, w2, tau, offs, k1, n1, n2, two, n3, n4):
    d_k1 = unpack_weight(d_words, d_scales)[np.arange(K)[:, None], runs(k1, K)]
    xq = unpack_weight(x_words, x_scales)[:, unstriped(offs)]
    s = 0.0625 * (d_k1.T @ xq)
    st = s - s[:, unstriped(n1)]
    z = f64(gn) * (st / (np.abs(st[:, unstriped(n2)]) + 0.5))
    x_two = unpack_weight(x_words, x_scales)[:, unstriped(two)]
    h = mxq(f64(w1), 0, "e4m3").T @ mxq(z, 0, "e4m3") + mxq(f64(w2), 0, "e4m3").T @ x_two
    sz = np.abs(h)
    ea = np.exp(-1.0 * (f64(tau) * sz[:, unstriped(n3)]))
    return (h - h[:, unstriped(n4)]) * ea

@@ -1,0 +1,178 @@
+from contextlib import ExitStack
+
+import concourse.mybir as mybir
+
+F32 = mybir.dt.float32
+BF16 = mybir.dt.bfloat16
+I32 = mybir.dt.int32
+U32 = mybir.dt.uint32
+U16 = mybir.dt.uint16
+U8 = mybir.dt.uint8
+FP8X4 = mybir.dt.float8_e4m3fn_x4
+ALU = mybir.AluOpType
+ACT = mybir.ActivationFunctionType
+
+P = 128
+T = 2048
+S = 256
+H = 512
+PACK = 4
+SPARE = 16
+W_BYTES = PACK * H * 4
+FLOPS = 3 * 2 * 512 * 512 * 256
+W_ON_SCALAR = 5
+
+
+def tile_picked_kmixhopnela_none_p_kernel(tc, x_words, x_scales, d_words, d_scales, gn, w1, w2, tau, offs, k1, n1, n2, two, n3, n4, out):
+    nc = tc.nc
+    with ExitStack() as ctx:
+        keep = ctx.enter_context(tc.tile_pool(name="keep", bufs=1))
+        shared = ctx.enter_context(tc.tile_pool(name="shared", bufs=1))
+        psum = ctx.enter_context(tc.psum_pool(name="psum", bufs=1))
+
+        def load_list(name, src, n):
+            lst = keep.tile([P, n // 16], U16, name=name)
+            nc.sync.dma_start(lst[:], src)
+            return lst
+
+        d_byte_table = keep.tile([P, T], U8, name="d_byte_table")
+        x_byte_table = keep.tile([P, T], U8, name="x_byte_table")
+        d_word_table = keep.tile([P, T], U32, name="d_word_table", tag="slot_w1")
+        x_word_table = keep.tile([P, T], U32, name="x_word_table")
+        nc.vector.memset(d_byte_table[:, : T // 2].bitcast(I32), 0)
+        nc.gpsimd.memset(d_byte_table[:, T // 2 :].bitcast(I32), 0)
+        nc.gpsimd.memset(x_byte_table[:].bitcast(I32), 0)
+        nc.sync.dma_start(d_byte_table[0:P:8, :].bitcast(I32), d_scales[0].bitcast(I32))
+        k1_list = load_list("k1_list", k1, H)
+        offs_list = load_list("offs_list", offs, S)
+        two_list = load_list("two_list", two, S)
+        n1_list = load_list("n1_list", n1, S)
+        n2_list = load_list("n2_list", n2, S)
+        nc.sync.dma_start(d_word_table[:].bitcast(I32), d_words[0].rearrange("p c r -> p (c r)").bitcast(I32))
+        nc.scalar.dma_start(x_byte_table[0:P:8, :].bitcast(I32), x_scales[0].bitcast(I32))
+        n3_list = load_list("n3_list", n3, S)
+        n4_list = load_list("n4_list", n4, S)
+        nc.sync.dma_start(x_word_table[:].bitcast(I32), x_words[0].rearrange("p c r -> p (c r)").bitcast(I32))
+        gain = keep.tile([P, PACK], F32, name="gain")
+        nc.scalar.dma_start(gain[:], gn.rearrange("(p t) o -> p (t o)", t=PACK))
+        rate = keep.tile([P, PACK], F32, name="rate")
+        with nc.allow_non_contiguous_dma(reason="one rate a row, four rows a partition"):
+            nc.gpsimd.dma_start(rate[:], tau.rearrange("(t p) o -> p (t o)", p=P))
+
+        neg_win = [keep.tile([P, S + SPARE], F32, name=f"neg_win{t}") for t in range(PACK)]
+        inv_win = [keep.tile([P, S + SPARE], F32, name=f"inv_win{t}") for t in range(PACK)]
+        for win in neg_win + inv_win:
+            nc.gpsimd.memset(win[:, S:], 0.0)
+
+        d_bytes = keep.tile([P, H], U8, name="d_bytes")
+        x_bytes = shared.tile([P, 2 * S], U8, name="x_bytes", offset=W_BYTES - S)
+        picked_scales = keep.tile([P, H + 2 * S], U8, name="picked_scales", align_bytes=64)
+        spread_scales = keep.tile([P, H + 2 * S], U8, name="spread_scales")
+        nc.gpsimd.memset(picked_scales[:].bitcast(I32), 0)
+        nc.vector.tensor_copy(d_bytes[:], d_byte_table[:].indirect(k1_list[:]))
+        nc.vector.tensor_copy(spread_scales[:, :H].rearrange("p (t m) -> p m t", t=PACK), d_bytes[:].rearrange("p (m t) -> p m t", t=PACK))
+        nc.vector.tensor_copy(x_bytes[:, :S], x_byte_table[:].indirect(offs_list[:]))
+        nc.vector.tensor_copy(x_bytes[:, S:], x_byte_table[:].indirect(two_list[:]))
+        nc.vector.tensor_copy(spread_scales[:, H:].bitcast(I32), x_bytes[:].bitcast(I32))
+        for q in range(0, P, 32):
+            nc.sync.dma_start(picked_scales[q : q + 4, :].bitcast(I32), spread_scales[q : q + 32 : 8, :].bitcast(I32))
+        xq_scales = picked_scales[:, H : H + S]
+        x2_scales = picked_scales[:, H + S :]
+        d_picked = shared.tile([P, H], U32, name="d_picked", offset=W_BYTES)
+        key_codes = keep.tile([P, H], U32, name="key_codes", align_bytes=64)
+        nc.vector.tensor_copy(d_picked[:], d_word_table[:].indirect(k1_list[:]))
+        nc.vector.tensor_copy(key_codes[:].rearrange("p (t m) -> p m t", t=PACK), d_picked[:].rearrange("p (m t) -> p m t", t=PACK))
+        xq_codes = keep.tile([P, S], U32, name="xq_codes", align_bytes=64)
+        nc.vector.tensor_copy(xq_codes[:], x_word_table[:].indirect(offs_list[:]))
+
+        w_raw = []
+        w_raw.append(shared.tile([P, PACK, H], F32, name="w2_raw", offset=0))
+        w_raw.append(keep.tile([P, PACK, H], F32, name="w1_raw", tag="slot_w1"))
+        for raw, w in zip(w_raw, (w2, w1)):
+            nc.sync.dma_start(raw[:], w.rearrange("(p j) c -> p j c", j=PACK))
+
+        gain_forms = keep.tile([P, 2 * PACK], F32, name="gain_forms")
+        neg_gain = gain_forms[:, :PACK]
+        safe_gain = gain_forms[:, PACK:]
+        inv_gain = keep.tile([P, PACK], F32, name="inv_gain")
+        neg_rate = keep.tile([P, PACK], F32, name="neg_rate")
+        nc.vector.tensor_scalar(neg_gain, gain[:], -0.0625, None, ALU.mult)
+        nc.vector.scalar_tensor_tensor(safe_gain, gain[:], 0.0, gain[:], ALU.is_equal, ALU.add)
+        nc.vector.reciprocal(inv_gain[:], safe_gain)
+        nc.gpsimd.tensor_scalar(neg_rate[:], rate[:], -1.0, 0.0, ALU.mult, ALU.add)
+        half = keep.tile([P, 1], F32, name="half")
+        nc.gpsimd.memset(half[:], 0.5)
+
+        warm_root = keep.tile([P, 1], F32, name="warm_root")
+        nc.scalar.activation(warm_root[:], half[:], ACT.Abs_reciprocal_sqrt)
+        s_bank = [psum.tile([P, S], F32, name=f"s_bank{t}") for t in range(PACK)]
+        h_bank = [psum.tile([P, S], F32, name=f"h_bank{t}") for t in range(PACK)]
+        pos = [keep.tile([P, S], F32, name=f"pos{t}") for t in range(PACK)]
+        diff = [keep.tile([P, S], F32, name=f"diff{t}") for t in range(PACK)]
+        size = [keep.tile([P, S], F32, name=f"size{t}") for t in range(PACK)]
+        sq = [keep.tile([P, S], F32, name=f"sq{t}") for t in range(PACK)]
+        z_rows = keep.tile([P, PACK, S], F32, name="z_rows")
+        for t in range(PACK):
+            cols = slice(t * P, (t + 1) * P)
+            nc.tensor.matmul_mx(s_bank[t][:], lhsT=key_codes[:, cols].bitcast(FP8X4), lhsT_scale=picked_scales[:, cols],
+                                rhs=xq_codes[:].bitcast(FP8X4), rhs_scale=xq_scales, start=True, stop=True)
+        for t in range(PACK):
+            nc.scalar.activation(neg_win[t][:, :S], s_bank[t][:], ACT.Copy, scale=gain_forms[:, t : t + 1])
+            nc.vector.tensor_scalar(pos[t][:], neg_win[t][:, :S], -1.0, None, ALU.mult)
+            nc.vector.tensor_tensor(diff[t][:], neg_win[t][:].indirect(n1_list[:]), pos[t][:], ALU.add)
+        for t in range(PACK):
+            nc.scalar.activation(size[t][:], diff[t][:], ACT.Abs, scale=inv_gain[:, t : t + 1])
+            nc.scalar.activation(sq[t][:], size[t][:], ACT.Square, bias=half[:])
+            nc.scalar.activation(inv_win[t][:, :S], sq[t][:], ACT.Abs_reciprocal_sqrt)
+            nc.vector.tensor_tensor(z_rows[:, t, :], inv_win[t][:].indirect(n2_list[:]), diff[t][:], ALU.mult)
+        z_bf = keep.tile([P, S, PACK], BF16, name="z_bf", align_bytes=64)
+        z_codes = keep.tile([P, S], U32, name="z_codes", align_bytes=64)
+        z_scales = keep.tile([P, S], U8, name="z_scales", align_bytes=64)
+        nc.vector.tensor_copy(z_bf[:].rearrange("p (c i) t -> p c t i", i=4), z_rows[:].rearrange("p t (c i) -> p c t i", i=4))
+        nc.vector.quantize_mx(z_codes[:].bitcast(FP8X4), z_scales[:], z_bf[:].rearrange("p c t -> p (c t)"))
+
+        x2_codes = keep.tile([P, S], U32, name="x2_codes", align_bytes=64)
+        nc.vector.tensor_copy(x2_codes[:], x_word_table[:].indirect(two_list[:]))
+
+        w_codes = []
+        w_scales = []
+        for i, raw in enumerate(w_raw):
+            for t in range(PACK):
+                grouped = keep.tile([P, P, PACK], BF16, name=f"w_bf{i}{t}", align_bytes=64)
+                codes = keep.tile([P, P], U32, name=f"w_codes{i}{t}", align_bytes=64)
+                scales = keep.tile([P, P], U8, name=f"w_scales{i}{t}", align_bytes=64)
+                dst = grouped[:].rearrange("p (c i) j -> p c j i", i=4)
+                src = raw[:, :, t * P : (t + 1) * P].rearrange("p j (c i) -> p c j i", i=4)
+                if i * PACK + t < W_ON_SCALAR:
+                    nc.scalar.copy(dst, src)
+                else:
+                    nc.vector.tensor_copy(dst, src)
+                if i * PACK + t == W_ON_SCALAR - 1:
+                    warm_exp = keep.tile([P, 1], F32, name="warm_exp")
+                    nc.scalar.activation(warm_exp[:], grouped[:, 0, 0:1], ACT.Exp, scale=0.0, bias=inv_win[PACK - 1][:, 0:1])
+                nc.vector.quantize_mx(codes[:].bitcast(FP8X4), scales[:], grouped[:].rearrange("p c j -> p (c j)"))
+                w_codes.append(codes)
+                w_scales.append(scales)
+
+        for t in range(PACK):
+            nc.tensor.matmul_mx(h_bank[t][:], lhsT=w_codes[t][:].bitcast(FP8X4), lhsT_scale=w_scales[t][:],
+                                rhs=x2_codes[:].bitcast(FP8X4), rhs_scale=x2_scales, start=True, stop=False)
+        for t in range(PACK):
+            nc.tensor.matmul_mx(h_bank[t][:], lhsT=w_codes[PACK + t][:].bitcast(FP8X4), lhsT_scale=w_scales[PACK + t][:],
+                                rhs=z_codes[:].bitcast(FP8X4), rhs_scale=z_scales[:], start=False, stop=True)
+
+        for t in range(PACK):
+            size_win = keep.tile([P, 2 * S], F32, name=f"size_win{t}")
+            gate = keep.tile([P, S], F32, name=f"gate{t}")
+            h_diff = keep.tile([P, S], F32, name=f"h_diff{t}")
+            result = keep.tile([P, S], F32, name=f"result{t}")
+            if t == 0:
+                nc.vector.tensor_scalar(neg_win[t][:, :S], h_bank[t][:], -1.0, None, ALU.mult)
+            else:
+                nc.scalar.activation(neg_win[t][:, :S], h_bank[t][:], ACT.Copy, scale=-1.0)
+            nc.scalar.activation(size_win[:, :S], h_bank[t][:], ACT.Abs)
+            nc.vector.tensor_scalar(size_win[:, S:], neg_win[t][:, :S], -1.0, None, ALU.mult)
+            nc.scalar.activation(gate[:], size_win[:].indirect(n3_list[:]), ACT.Exp, scale=neg_rate[:, t : t + 1])
+            nc.vector.tensor_tensor(h_diff[:], neg_win[t][:].indirect(n4_list[:]), size_win[:, S:], ALU.add)
+            nc.vector.tensor_tensor(result[:], h_diff[:], gate[:], ALU.mult)
+            nc.sync.dma_start(out[t * P : (t + 1) * P, :], result[:])

@@ -18,9 +18,9 @@ S = 256
 H = 512
 PACK = 4
 SPARE = 16
-W_BYTES = PACK * H * 4
+HALF = H // 2
+W_BYTES = PACK * HALF * 4
 FLOPS = 3 * 2 * 512 * 512 * 256
-W_ON_SCALAR = 5
 
 
 def tile_picked_kmixhopnela_none_p_kernel(tc, x_words, x_scales, d_words, d_scales, gn, w1, w2, tau, offs, k1, n1, n2, two, n3, n4, out):
@@ -52,6 +52,9 @@ def tile_picked_kmixhopnela_none_p_kernel(tc, x_words, x_scales, d_words, d_scal
         nc.scalar.dma_start(x_byte_table[0:P:8, :].bitcast(I32), x_scales[0].bitcast(I32))
         n3_list = load_list("n3_list", n3, S)
         n4_list = load_list("n4_list", n4, S)
+        w2_rows = w2.rearrange("(p j) c -> p j c", j=PACK)
+        w2_first = keep.tile([P, PACK, HALF], F32, name="w2_first")
+        nc.sync.dma_start(w2_first[:], w2_rows[:, :, :HALF])
         nc.sync.dma_start(x_word_table[:].bitcast(I32), x_words[0].rearrange("p c r -> p (c r)").bitcast(I32))
         gain = keep.tile([P, PACK], F32, name="gain")
         nc.scalar.dma_start(gain[:], gn.rearrange("(p t) o -> p (t o)", t=PACK))
@@ -85,11 +88,10 @@ def tile_picked_kmixhopnela_none_p_kernel(tc, x_words, x_scales, d_words, d_scal
         xq_codes = keep.tile([P, S], U32, name="xq_codes", align_bytes=64)
         nc.vector.tensor_copy(xq_codes[:], x_word_table[:].indirect(offs_list[:]))
 
-        w_raw = []
-        w_raw.append(shared.tile([P, PACK, H], F32, name="w2_raw", offset=0))
-        w_raw.append(keep.tile([P, PACK, H], F32, name="w1_raw", tag="slot_w1"))
-        for raw, w in zip(w_raw, (w2, w1)):
-            nc.sync.dma_start(raw[:], w.rearrange("(p j) c -> p j c", j=PACK))
+        w2_second = shared.tile([P, PACK, HALF], F32, name="w2_second", offset=0)
+        nc.sync.dma_start(w2_second[:], w2_rows[:, :, HALF:])
+        w1_raw = keep.tile([P, PACK, H], F32, name="w1_raw", tag="slot_w1")
+        nc.sync.dma_start(w1_raw[:], w1.rearrange("(p j) c -> p j c", j=PACK))
 
         gain_forms = keep.tile([P, 2 * PACK], F32, name="gain_forms")
         neg_gain = gain_forms[:, :PACK]
@@ -110,7 +112,7 @@ def tile_picked_kmixhopnela_none_p_kernel(tc, x_words, x_scales, d_words, d_scal
         pos = [keep.tile([P, S], F32, name=f"pos{t}") for t in range(PACK)]
         diff = [keep.tile([P, S], F32, name=f"diff{t}") for t in range(PACK)]
         size = [keep.tile([P, S], F32, name=f"size{t}") for t in range(PACK)]
-        sq = [keep.tile([P, S], F32, name=f"sq{t}") for t in range(PACK)]
+        sq = [keep.tile([P, S], F32, name=f"sq{t}", tag=f"slot_sq{t}", align_bytes=64) for t in range(PACK)]
         z_rows = keep.tile([P, PACK, S], F32, name="z_rows")
         for t in range(PACK):
             cols = slice(t * P, (t + 1) * P)
@@ -134,31 +136,34 @@ def tile_picked_kmixhopnela_none_p_kernel(tc, x_words, x_scales, d_words, d_scal
         x2_codes = keep.tile([P, S], U32, name="x2_codes", align_bytes=64)
         nc.vector.tensor_copy(x2_codes[:], x_word_table[:].indirect(two_list[:]))
 
-        w_codes = []
-        w_scales = []
-        for i, raw in enumerate(w_raw):
-            for t in range(PACK):
-                grouped = keep.tile([P, P, PACK], BF16, name=f"w_bf{i}{t}", align_bytes=64)
-                codes = keep.tile([P, P], U32, name=f"w_codes{i}{t}", align_bytes=64)
-                scales = keep.tile([P, P], U8, name=f"w_scales{i}{t}", align_bytes=64)
-                dst = grouped[:].rearrange("p (c i) j -> p c j i", i=4)
-                src = raw[:, :, t * P : (t + 1) * P].rearrange("p j (c i) -> p c j i", i=4)
-                if i * PACK + t < W_ON_SCALAR:
-                    nc.scalar.copy(dst, src)
-                else:
-                    nc.vector.tensor_copy(dst, src)
-                if i * PACK + t == W_ON_SCALAR - 1:
-                    warm_exp = keep.tile([P, 1], F32, name="warm_exp")
-                    nc.scalar.activation(warm_exp[:], grouped[:, 0, 0:1], ACT.Exp, scale=0.0, bias=inv_win[PACK - 1][:, 0:1])
-                nc.vector.quantize_mx(codes[:].bitcast(FP8X4), scales[:], grouped[:].rearrange("p c j -> p (c j)"))
-                w_codes.append(codes)
-                w_scales.append(scales)
+        w1_codes = keep.tile([P, H], U32, name="w1_codes", align_bytes=64)
+        w2_codes = keep.tile([P, H], U32, name="w2_codes", align_bytes=64)
+        w1_scales = keep.tile([P, H], U8, name="w1_scales", align_bytes=64)
+        w2_scales = keep.tile([P, H], U8, name="w2_scales", align_bytes=64)
+
+        def quantise(name, raw, copy, step, codes, scales, tag):
+            width = raw.shape[2]
+            grouped = keep.tile([P, width, PACK], BF16, name=name, tag=tag, align_bytes=64)
+            for c in range(0, width, step):
+                copy(grouped[:, c : c + step, :].rearrange("p (c i) j -> p c j i", i=4),
+                     raw[:, :, c : c + step].rearrange("p j (c i) -> p c j i", i=4))
+            nc.vector.quantize_mx(codes.bitcast(FP8X4), scales, grouped[:].rearrange("p c j -> p (c j)"))
+            return grouped
+
+        on_vector, on_scalar = nc.vector.tensor_copy, nc.scalar.copy
+        quantise("w2_bf01", w2_first[:], on_scalar, HALF, w2_codes[:, :HALF], w2_scales[:, :HALF], "w2_bf01")
+        quantise("w1_bf01", w1_raw[:, :, :HALF], on_vector, P, w1_codes[:, :HALF], w1_scales[:, :HALF], "w1_bf01")
+        quantise("w2_bf2", w2_second[:, :, :P], on_vector, P, w2_codes[:, HALF : HALF + P], w2_scales[:, HALF : HALF + P], "w2_bf2")
+        last = quantise("w1_bf23", w1_raw[:, :, HALF:], on_scalar, HALF, w1_codes[:, HALF:], w1_scales[:, HALF:], "slot_sq3")
+        quantise("w2_bf3", w2_second[:, :, P:], on_scalar, P, w2_codes[:, HALF + P :], w2_scales[:, HALF + P :], "slot_sq2")
+        warm_exp = keep.tile([P, 1], F32, name="warm_exp")
+        nc.scalar.activation(warm_exp[:], last[:, 0, 0:1], ACT.Exp, scale=0.0, bias=inv_win[PACK - 1][:, 0:1])
 
         for t in range(PACK):
-            nc.tensor.matmul_mx(h_bank[t][:], lhsT=w_codes[t][:].bitcast(FP8X4), lhsT_scale=w_scales[t][:],
+            cols = slice(t * P, (t + 1) * P)
+            nc.tensor.matmul_mx(h_bank[t][:], lhsT=w2_codes[:, cols].bitcast(FP8X4), lhsT_scale=w2_scales[:, cols],
                                 rhs=x2_codes[:].bitcast(FP8X4), rhs_scale=x2_scales, start=True, stop=False)
-        for t in range(PACK):
-            nc.tensor.matmul_mx(h_bank[t][:], lhsT=w_codes[PACK + t][:].bitcast(FP8X4), lhsT_scale=w_scales[PACK + t][:],
+            nc.tensor.matmul_mx(h_bank[t][:], lhsT=w1_codes[:, cols].bitcast(FP8X4), lhsT_scale=w1_scales[:, cols],
                                 rhs=z_codes[:].bitcast(FP8X4), rhs_scale=z_scales[:], start=False, stop=True)
 
         for t in range(PACK):
@@ -166,7 +171,7 @@ def tile_picked_kmixhopnela_none_p_kernel(tc, x_words, x_scales, d_words, d_scal
             gate = keep.tile([P, S], F32, name=f"gate{t}")
             h_diff = keep.tile([P, S], F32, name=f"h_diff{t}")
             result = keep.tile([P, S], F32, name=f"result{t}")
-            if t == 0:
+            if t < 2:
                 nc.vector.tensor_scalar(neg_win[t][:, :S], h_bank[t][:], -1.0, None, ALU.mult)
             else:
                 nc.scalar.activation(neg_win[t][:, :S], h_bank[t][:], ACT.Copy, scale=-1.0)

@@ -19,7 +19,6 @@ H = 512
 PACK = 4
 SPARE = 16
 HALF = H // 2
-W_BYTES = PACK * HALF * 4
 FLOPS = 3 * 2 * 512 * 512 * 256
 
 
@@ -27,7 +26,6 @@ def tile_picked_kmixhopnela_none_p_kernel(tc, x_words, x_scales, d_words, d_scal
     nc = tc.nc
     with ExitStack() as ctx:
         keep = ctx.enter_context(tc.tile_pool(name="keep", bufs=1))
-        shared = ctx.enter_context(tc.tile_pool(name="shared", bufs=1))
         psum = ctx.enter_context(tc.psum_pool(name="psum", bufs=1))
 
         def load_list(name, src, n):
@@ -36,7 +34,7 @@ def tile_picked_kmixhopnela_none_p_kernel(tc, x_words, x_scales, d_words, d_scal
             return lst
 
         d_byte_table = keep.tile([P, T], U8, name="d_byte_table")
-        x_byte_table = keep.tile([P, T], U8, name="x_byte_table")
+        x_byte_table = keep.tile([P, T], U8, name="x_byte_table", tag="slot_keys")
         d_word_table = keep.tile([P, T], U32, name="d_word_table", tag="slot_w1")
         x_word_table = keep.tile([P, T], U32, name="x_word_table")
         nc.vector.memset(d_byte_table[:, : T // 2].bitcast(I32), 0)
@@ -45,22 +43,19 @@ def tile_picked_kmixhopnela_none_p_kernel(tc, x_words, x_scales, d_words, d_scal
         nc.sync.dma_start(d_byte_table[0:P:8, :].bitcast(I32), d_scales[0].bitcast(I32))
         k1_list = load_list("k1_list", k1, H)
         offs_list = load_list("offs_list", offs, S)
+        nc.sync.dma_start(d_word_table[:].bitcast(I32), d_words[0].rearrange("p c r -> p (c r)").bitcast(I32))
+        nc.scalar.dma_start(x_byte_table[0:P:8, :].bitcast(I32), x_scales[0].bitcast(I32))
         two_list = load_list("two_list", two, S)
         n1_list = load_list("n1_list", n1, S)
         n2_list = load_list("n2_list", n2, S)
-        nc.sync.dma_start(d_word_table[:].bitcast(I32), d_words[0].rearrange("p c r -> p (c r)").bitcast(I32))
-        nc.scalar.dma_start(x_byte_table[0:P:8, :].bitcast(I32), x_scales[0].bitcast(I32))
-        n3_list = load_list("n3_list", n3, S)
-        n4_list = load_list("n4_list", n4, S)
+        nc.sync.dma_start(x_word_table[:].bitcast(I32), x_words[0].rearrange("p c r -> p (c r)").bitcast(I32))
         w2_rows = w2.rearrange("(p j) c -> p j c", j=PACK)
         w2_first = keep.tile([P, PACK, HALF], F32, name="w2_first")
         nc.sync.dma_start(w2_first[:], w2_rows[:, :, :HALF])
-        nc.sync.dma_start(x_word_table[:].bitcast(I32), x_words[0].rearrange("p c r -> p (c r)").bitcast(I32))
+        n3_list = load_list("n3_list", n3, S)
+        n4_list = load_list("n4_list", n4, S)
         gain = keep.tile([P, PACK], F32, name="gain")
         nc.scalar.dma_start(gain[:], gn.rearrange("(p t) o -> p (t o)", t=PACK))
-        rate = keep.tile([P, PACK], F32, name="rate")
-        with nc.allow_non_contiguous_dma(reason="one rate a row, four rows a partition"):
-            nc.gpsimd.dma_start(rate[:], tau.rearrange("(t p) o -> p (t o)", p=P))
 
         neg_win = [keep.tile([P, S + SPARE], F32, name=f"neg_win{t}") for t in range(PACK)]
         inv_win = [keep.tile([P, S + SPARE], F32, name=f"inv_win{t}") for t in range(PACK)]
@@ -68,30 +63,34 @@ def tile_picked_kmixhopnela_none_p_kernel(tc, x_words, x_scales, d_words, d_scal
             nc.gpsimd.memset(win[:, S:], 0.0)
 
         d_bytes = keep.tile([P, H], U8, name="d_bytes")
-        x_bytes = shared.tile([P, 2 * S], U8, name="x_bytes", offset=W_BYTES - S)
+        x_bytes = keep.tile([P, 2 * S], U8, name="x_bytes", tag="slot_w2")
         picked_scales = keep.tile([P, H + 2 * S], U8, name="picked_scales", align_bytes=64)
         spread_scales = keep.tile([P, H + 2 * S], U8, name="spread_scales")
         nc.gpsimd.memset(picked_scales[:].bitcast(I32), 0)
         nc.vector.tensor_copy(d_bytes[:], d_byte_table[:].indirect(k1_list[:]))
-        nc.vector.tensor_copy(spread_scales[:, :H].rearrange("p (t m) -> p m t", t=PACK), d_bytes[:].rearrange("p (m t) -> p m t", t=PACK))
         nc.vector.tensor_copy(x_bytes[:, :S], x_byte_table[:].indirect(offs_list[:]))
         nc.vector.tensor_copy(x_bytes[:, S:], x_byte_table[:].indirect(two_list[:]))
+        nc.vector.tensor_copy(spread_scales[:, :H].rearrange("p (t m) -> p t m", t=PACK), d_bytes[:].rearrange("p (m t) -> p t m", t=PACK))
         nc.vector.tensor_copy(spread_scales[:, H:].bitcast(I32), x_bytes[:].bitcast(I32))
         for q in range(0, P, 32):
             nc.sync.dma_start(picked_scales[q : q + 4, :].bitcast(I32), spread_scales[q : q + 32 : 8, :].bitcast(I32))
         xq_scales = picked_scales[:, H : H + S]
         x2_scales = picked_scales[:, H + S :]
-        d_picked = shared.tile([P, H], U32, name="d_picked", offset=W_BYTES)
+        d_picked = keep.tile([P, H], U32, name="d_picked", tag="slot_keys")
         key_codes = keep.tile([P, H], U32, name="key_codes", align_bytes=64)
         nc.vector.tensor_copy(d_picked[:], d_word_table[:].indirect(k1_list[:]))
-        nc.vector.tensor_copy(key_codes[:].rearrange("p (t m) -> p m t", t=PACK), d_picked[:].rearrange("p (m t) -> p m t", t=PACK))
+        nc.vector.tensor_copy(key_codes[:].rearrange("p (t b i) -> p b t i", t=PACK, i=4), d_picked[:].rearrange("p (b i t) -> p b t i", t=PACK, i=4))
         xq_codes = keep.tile([P, S], U32, name="xq_codes", align_bytes=64)
         nc.vector.tensor_copy(xq_codes[:], x_word_table[:].indirect(offs_list[:]))
 
-        w2_second = shared.tile([P, PACK, HALF], F32, name="w2_second", offset=0)
+        w2_second = keep.tile([P, PACK, HALF], F32, name="w2_second", tag="slot_w2")
         nc.sync.dma_start(w2_second[:], w2_rows[:, :, HALF:])
         w1_raw = keep.tile([P, PACK, H], F32, name="w1_raw", tag="slot_w1")
         nc.sync.dma_start(w1_raw[:], w1.rearrange("(p j) c -> p j c", j=PACK))
+
+        rate = keep.tile([P, PACK], F32, name="rate", tag="slot_keys")
+        with nc.allow_non_contiguous_dma(reason="one rate a row, four rows a partition"):
+            nc.sync.dma_start(rate[:], tau.rearrange("(t p) o -> p (t o)", p=P))
 
         gain_forms = keep.tile([P, 2 * PACK], F32, name="gain_forms")
         neg_gain = gain_forms[:, :PACK]

@@ -13,170 +13,219 @@ ALU = mybir.AluOpType
 ACT = mybir.ActivationFunctionType
 
 P = 128
-T = 2048
-S = 256
-H = 512
 PACK = 4
+TABLE = 2048
+PICKS = 256
+ROWS = 512
+HALF = ROWS // 2
+GROUP = 16
+BLOCK = 8
+QUADRANT = 32
+LINE = 4
 SPARE = 16
-HALF = H // 2
-FLOPS = 3 * 2 * 512 * 512 * 256
+FLOPS = 3 * 2 * ROWS * ROWS * PICKS
 
 
-def tile_picked_kmixhopnela_none_p_kernel(tc, x_words, x_scales, d_words, d_scales, gn, w1, w2, tau, offs, k1, n1, n2, two, n3, n4, out):
+def tile_picked_kmixhopnela_none_p_kernel(
+    tc, x_words, x_scales, d_words, d_scales, gn, w1, w2, tau, offs, k1, n1, n2, two, n3, n4, out
+):
     nc = tc.nc
     with ExitStack() as ctx:
         keep = ctx.enter_context(tc.tile_pool(name="keep", bufs=1))
         psum = ctx.enter_context(tc.psum_pool(name="psum", bufs=1))
 
-        def load_list(name, src, n):
-            lst = keep.tile([P, n // 16], U16, name=name)
+        def load_list(name, src, entries):
+            lst = keep.tile([P, entries // GROUP], U16, name=name)
             nc.sync.dma_start(lst[:], src)
             return lst
 
-        d_byte_table = keep.tile([P, T], U8, name="d_byte_table")
-        x_byte_table = keep.tile([P, T], U8, name="x_byte_table", tag="slot_keys")
-        d_word_table = keep.tile([P, T], U32, name="d_word_table", tag="slot_w1")
-        x_word_table = keep.tile([P, T], U32, name="x_word_table")
-        nc.vector.memset(d_byte_table[:, : T // 2].bitcast(I32), 0)
-        nc.gpsimd.memset(d_byte_table[:, T // 2 :].bitcast(I32), 0)
+        d_byte_table = keep.tile([P, TABLE], U8, name="d_byte_table")
+        x_byte_table = keep.tile([P, TABLE], U8, name="x_byte_table", tag="after_x_bytes")
+        d_word_table = keep.tile([P, TABLE], U32, name="d_word_table", tag="after_d_words")
+        x_word_table = keep.tile([P, TABLE], U32, name="x_word_table")
+
+        nc.vector.memset(d_byte_table[:, : TABLE // 2].bitcast(I32), 0)
+        nc.gpsimd.memset(d_byte_table[:, TABLE // 2 :].bitcast(I32), 0)
         nc.gpsimd.memset(x_byte_table[:].bitcast(I32), 0)
-        nc.sync.dma_start(d_byte_table[0:P:8, :].bitcast(I32), d_scales[0].bitcast(I32))
-        k1_list = load_list("k1_list", k1, H)
-        offs_list = load_list("offs_list", offs, S)
+        nc.sync.dma_start(d_byte_table[0:P:BLOCK, :].bitcast(I32), d_scales[0].bitcast(I32))
+        k1_list = load_list("k1_list", k1, ROWS)
+        offs_list = load_list("offs_list", offs, PICKS)
         nc.sync.dma_start(d_word_table[:].bitcast(I32), d_words[0].rearrange("p c r -> p (c r)").bitcast(I32))
-        nc.scalar.dma_start(x_byte_table[0:P:8, :].bitcast(I32), x_scales[0].bitcast(I32))
-        two_list = load_list("two_list", two, S)
-        n1_list = load_list("n1_list", n1, S)
-        n2_list = load_list("n2_list", n2, S)
+        nc.scalar.dma_start(x_byte_table[0:P:BLOCK, :].bitcast(I32), x_scales[0].bitcast(I32))
+        two_list = load_list("two_list", two, PICKS)
+        n1_list = load_list("n1_list", n1, PICKS)
+        n2_list = load_list("n2_list", n2, PICKS)
+        n3_list = load_list("n3_list", n3, PICKS)
         nc.sync.dma_start(x_word_table[:].bitcast(I32), x_words[0].rearrange("p c r -> p (c r)").bitcast(I32))
         w2_rows = w2.rearrange("(p j) c -> p j c", j=PACK)
         w2_first = keep.tile([P, PACK, HALF], F32, name="w2_first")
         nc.sync.dma_start(w2_first[:], w2_rows[:, :, :HALF])
-        n3_list = load_list("n3_list", n3, S)
-        n4_list = load_list("n4_list", n4, S)
+        n4_list = load_list("n4_list", n4, PICKS)
         gain = keep.tile([P, PACK], F32, name="gain")
         nc.scalar.dma_start(gain[:], gn.rearrange("(p t) o -> p (t o)", t=PACK))
 
-        neg_win = [keep.tile([P, S + SPARE], F32, name=f"neg_win{t}") for t in range(PACK)]
-        inv_win = [keep.tile([P, S + SPARE], F32, name=f"inv_win{t}") for t in range(PACK)]
-        for win in neg_win + inv_win:
-            nc.gpsimd.memset(win[:, S:], 0.0)
+        negated = [keep.tile([P, PICKS + SPARE], F32, name=f"negated{t}") for t in range(PACK)]
+        inverse = [keep.tile([P, PICKS + SPARE], F32, name=f"inverse{t}") for t in range(PACK)]
+        for window in negated + inverse:
+            nc.gpsimd.memset(window[:, PICKS:], 0.0)
 
-        d_bytes = keep.tile([P, H], U8, name="d_bytes")
-        x_bytes = keep.tile([P, 2 * S], U8, name="x_bytes", tag="slot_w2")
-        picked_scales = keep.tile([P, H + 2 * S], U8, name="picked_scales", align_bytes=64)
-        spread_scales = keep.tile([P, H + 2 * S], U8, name="spread_scales")
-        nc.gpsimd.memset(picked_scales[:].bitcast(I32), 0)
+        d_bytes = keep.tile([P, ROWS], U8, name="d_bytes")
+        x_bytes = keep.tile([P, 2 * PICKS], U8, name="x_bytes", tag="after_x_copy")
+        picked_scales = keep.tile([P, ROWS + 2 * PICKS], U8, name="picked_scales", align_bytes=64)
         nc.vector.tensor_copy(d_bytes[:], d_byte_table[:].indirect(k1_list[:]))
-        nc.vector.tensor_copy(x_bytes[:, :S], x_byte_table[:].indirect(offs_list[:]))
-        nc.vector.tensor_copy(x_bytes[:, S:], x_byte_table[:].indirect(two_list[:]))
-        nc.vector.tensor_copy(spread_scales[:, :H].rearrange("p (t m) -> p t m", t=PACK), d_bytes[:].rearrange("p (m t) -> p t m", t=PACK))
-        nc.vector.tensor_copy(spread_scales[:, H:].bitcast(I32), x_bytes[:].bitcast(I32))
-        for q in range(0, P, 32):
-            nc.sync.dma_start(picked_scales[q : q + 4, :].bitcast(I32), spread_scales[q : q + 32 : 8, :].bitcast(I32))
-        xq_scales = picked_scales[:, H : H + S]
-        x2_scales = picked_scales[:, H + S :]
-        d_picked = keep.tile([P, H], U32, name="d_picked", tag="slot_keys")
-        key_codes = keep.tile([P, H], U32, name="key_codes", align_bytes=64)
+        nc.vector.tensor_copy(x_bytes[:, :PICKS], x_byte_table[:].indirect(offs_list[:]))
+        nc.vector.tensor_copy(x_bytes[:, PICKS:], x_byte_table[:].indirect(two_list[:]))
+        nc.vector.tensor_copy(
+            picked_scales[:, :ROWS].rearrange("p (t m) -> p t m", t=PACK),
+            d_bytes[:].rearrange("p (m t) -> p t m", t=PACK),
+        )
+        nc.vector.tensor_copy(picked_scales[:, ROWS:].bitcast(I32), x_bytes[:].bitcast(I32))
+        for r in range(1, QUADRANT // BLOCK):
+            nc.sync.dma_start(
+                picked_scales[r:P:QUADRANT, :].bitcast(I32),
+                picked_scales[BLOCK * r : P : QUADRANT, :].bitcast(I32),
+            )
+        xq_scales = picked_scales[:, ROWS : ROWS + PICKS]
+        x2_scales = picked_scales[:, ROWS + PICKS :]
+
+        d_picked = keep.tile([P, ROWS], U32, name="d_picked", tag="after_x_bytes")
+        key_codes = keep.tile([P, ROWS], U32, name="key_codes", align_bytes=64)
         nc.vector.tensor_copy(d_picked[:], d_word_table[:].indirect(k1_list[:]))
-        nc.vector.tensor_copy(key_codes[:].rearrange("p (t b i) -> p b t i", t=PACK, i=4), d_picked[:].rearrange("p (b i t) -> p b t i", t=PACK, i=4))
-        xq_codes = keep.tile([P, S], U32, name="xq_codes", align_bytes=64)
+        nc.vector.tensor_copy(
+            key_codes[:].rearrange("p (t b i) -> p b t i", t=PACK, i=LINE),
+            d_picked[:].rearrange("p (b i t) -> p b t i", t=PACK, i=LINE),
+        )
+        xq_codes = keep.tile([P, PICKS], U32, name="xq_codes", align_bytes=64)
         nc.vector.tensor_copy(xq_codes[:], x_word_table[:].indirect(offs_list[:]))
 
-        w2_second = keep.tile([P, PACK, HALF], F32, name="w2_second", tag="slot_w2")
+        w2_second = keep.tile([P, PACK, HALF], F32, name="w2_second", tag="after_x_copy")
         nc.sync.dma_start(w2_second[:], w2_rows[:, :, HALF:])
-        w1_raw = keep.tile([P, PACK, H], F32, name="w1_raw", tag="slot_w1")
+        w1_raw = keep.tile([P, PACK, ROWS], F32, name="w1_raw", tag="after_d_words")
         nc.sync.dma_start(w1_raw[:], w1.rearrange("(p j) c -> p j c", j=PACK))
-
-        rate = keep.tile([P, PACK], F32, name="rate", tag="slot_keys")
-        with nc.allow_non_contiguous_dma(reason="one rate a row, four rows a partition"):
+        rate = keep.tile([P, PACK], F32, name="rate", tag="after_x_bytes")
+        with nc.allow_non_contiguous_dma(reason="tau of row 128 t + p goes to [p, t]"):
             nc.sync.dma_start(rate[:], tau.rearrange("(t p) o -> p (t o)", p=P))
 
-        gain_forms = keep.tile([P, 2 * PACK], F32, name="gain_forms")
-        neg_gain = gain_forms[:, :PACK]
-        safe_gain = gain_forms[:, PACK:]
+        neg_gain = keep.tile([P, PACK], F32, name="neg_gain")
+        safe_gain = keep.tile([P, PACK], F32, name="safe_gain")
         inv_gain = keep.tile([P, PACK], F32, name="inv_gain")
         neg_rate = keep.tile([P, PACK], F32, name="neg_rate")
-        nc.vector.tensor_scalar(neg_gain, gain[:], -0.0625, None, ALU.mult)
-        nc.vector.scalar_tensor_tensor(safe_gain, gain[:], 0.0, gain[:], ALU.is_equal, ALU.add)
-        nc.vector.reciprocal(inv_gain[:], safe_gain)
+        nc.vector.tensor_scalar(neg_gain[:], gain[:], -1.0, None, ALU.mult)
+        nc.vector.scalar_tensor_tensor(safe_gain[:], gain[:], 0.0, gain[:], ALU.is_equal, ALU.add)
+        nc.vector.reciprocal(inv_gain[:], safe_gain[:])
         nc.gpsimd.tensor_scalar(neg_rate[:], rate[:], -1.0, 0.0, ALU.mult, ALU.add)
-        half = keep.tile([P, 1], F32, name="half")
-        nc.gpsimd.memset(half[:], 0.5)
+        eight = keep.tile([P, 1], F32, name="eight")
+        nc.gpsimd.memset(eight[:], 8.0)
 
         warm_root = keep.tile([P, 1], F32, name="warm_root")
-        nc.scalar.activation(warm_root[:], half[:], ACT.Abs_reciprocal_sqrt)
-        s_bank = [psum.tile([P, S], F32, name=f"s_bank{t}") for t in range(PACK)]
-        h_bank = [psum.tile([P, S], F32, name=f"h_bank{t}") for t in range(PACK)]
-        pos = [keep.tile([P, S], F32, name=f"pos{t}") for t in range(PACK)]
-        diff = [keep.tile([P, S], F32, name=f"diff{t}") for t in range(PACK)]
-        size = [keep.tile([P, S], F32, name=f"size{t}") for t in range(PACK)]
-        sq = [keep.tile([P, S], F32, name=f"sq{t}", tag=f"slot_sq{t}", align_bytes=64) for t in range(PACK)]
-        z_rows = keep.tile([P, PACK, S], F32, name="z_rows")
+        nc.scalar.activation(warm_root[:], eight[:], ACT.Abs_reciprocal_sqrt)
+
+        s_bank = [psum.tile([P, PICKS], F32, name=f"s_bank{t}") for t in range(PACK)]
+        h_bank = [psum.tile([P, PICKS], F32, name=f"h_bank{t}") for t in range(PACK)]
+        scored = [keep.tile([P, PICKS], F32, name=f"scored{t}") for t in range(PACK)]
+        diff = [keep.tile([P, PICKS], F32, name=f"diff{t}") for t in range(PACK)]
+        diff_size = [keep.tile([P, PICKS], F32, name=f"diff_size{t}") for t in range(PACK)]
+        squared = [
+            keep.tile([P, PICKS], F32, name=f"squared{t}", tag=f"after_root{t}", align_bytes=64) for t in range(PACK)
+        ]
+        z_rows = keep.tile([P, PACK, PICKS], F32, name="z_rows")
         for t in range(PACK):
             cols = slice(t * P, (t + 1) * P)
-            nc.tensor.matmul_mx(s_bank[t][:], lhsT=key_codes[:, cols].bitcast(FP8X4), lhsT_scale=picked_scales[:, cols],
-                                rhs=xq_codes[:].bitcast(FP8X4), rhs_scale=xq_scales, start=True, stop=True)
+            nc.tensor.matmul_mx(
+                s_bank[t][:],
+                lhsT=key_codes[:, cols].bitcast(FP8X4),
+                lhsT_scale=picked_scales[:, cols],
+                rhs=xq_codes[:].bitcast(FP8X4),
+                rhs_scale=xq_scales,
+                start=True,
+                stop=True,
+            )
         for t in range(PACK):
-            nc.scalar.activation(neg_win[t][:, :S], s_bank[t][:], ACT.Copy, scale=gain_forms[:, t : t + 1])
-            nc.vector.tensor_scalar(pos[t][:], neg_win[t][:, :S], -1.0, None, ALU.mult)
-            nc.vector.tensor_tensor(diff[t][:], neg_win[t][:].indirect(n1_list[:]), pos[t][:], ALU.add)
+            nc.scalar.activation(negated[t][:, :PICKS], s_bank[t][:], ACT.Copy, scale=neg_gain[:, t : t + 1])
+            nc.scalar.activation(scored[t][:], s_bank[t][:], ACT.Copy, scale=gain[:, t : t + 1])
+            nc.vector.tensor_tensor(diff[t][:], negated[t][:].indirect(n1_list[:]), scored[t][:], ALU.add)
         for t in range(PACK):
-            nc.scalar.activation(size[t][:], diff[t][:], ACT.Abs, scale=inv_gain[:, t : t + 1])
-            nc.scalar.activation(sq[t][:], size[t][:], ACT.Square, bias=half[:])
-            nc.scalar.activation(inv_win[t][:, :S], sq[t][:], ACT.Abs_reciprocal_sqrt)
-            nc.vector.tensor_tensor(z_rows[:, t, :], inv_win[t][:].indirect(n2_list[:]), diff[t][:], ALU.mult)
-        z_bf = keep.tile([P, S, PACK], BF16, name="z_bf", align_bytes=64)
-        z_codes = keep.tile([P, S], U32, name="z_codes", align_bytes=64)
-        z_scales = keep.tile([P, S], U8, name="z_scales", align_bytes=64)
-        nc.vector.tensor_copy(z_bf[:].rearrange("p (c i) t -> p c t i", i=4), z_rows[:].rearrange("p t (c i) -> p c t i", i=4))
-        nc.vector.quantize_mx(z_codes[:].bitcast(FP8X4), z_scales[:], z_bf[:].rearrange("p c t -> p (c t)"))
+            nc.scalar.activation(diff_size[t][:], diff[t][:], ACT.Abs, scale=inv_gain[:, t : t + 1])
+            nc.scalar.activation(squared[t][:], diff_size[t][:], ACT.Square, bias=eight[:])
+            nc.scalar.activation(inverse[t][:, :PICKS], squared[t][:], ACT.Abs_reciprocal_sqrt)
+            nc.vector.tensor_tensor(z_rows[:, t, :], inverse[t][:].indirect(n2_list[:]), diff[t][:], ALU.mult)
 
-        x2_codes = keep.tile([P, S], U32, name="x2_codes", align_bytes=64)
+        z_grouped = keep.tile([P, PICKS, PACK], BF16, name="z_grouped", align_bytes=64)
+        z_codes = keep.tile([P, PICKS], U32, name="z_codes", align_bytes=64)
+        z_scales = keep.tile([P, PICKS], U8, name="z_scales", align_bytes=64)
+        nc.vector.tensor_copy(
+            z_grouped[:].rearrange("p (c i) t -> p c t i", i=LINE),
+            z_rows[:].rearrange("p t (c i) -> p c t i", i=LINE),
+        )
+        nc.vector.quantize_mx(z_codes[:].bitcast(FP8X4), z_scales[:], z_grouped[:].rearrange("p c t -> p (c t)"))
+
+        x2_codes = keep.tile([P, PICKS], U32, name="x2_codes", align_bytes=64)
         nc.vector.tensor_copy(x2_codes[:], x_word_table[:].indirect(two_list[:]))
 
-        w1_codes = keep.tile([P, H], U32, name="w1_codes", align_bytes=64)
-        w2_codes = keep.tile([P, H], U32, name="w2_codes", align_bytes=64)
-        w1_scales = keep.tile([P, H], U8, name="w1_scales", align_bytes=64)
-        w2_scales = keep.tile([P, H], U8, name="w2_scales", align_bytes=64)
+        w1_codes = keep.tile([P, ROWS], U32, name="w1_codes", align_bytes=64)
+        w2_codes = keep.tile([P, ROWS], U32, name="w2_codes", align_bytes=64)
+        w1_scales = keep.tile([P, ROWS], U8, name="w1_scales", align_bytes=64)
+        w2_scales = keep.tile([P, ROWS], U8, name="w2_scales", align_bytes=64)
 
         def quantise(name, raw, copy, step, codes, scales, tag):
             width = raw.shape[2]
             grouped = keep.tile([P, width, PACK], BF16, name=name, tag=tag, align_bytes=64)
             for c in range(0, width, step):
-                copy(grouped[:, c : c + step, :].rearrange("p (c i) j -> p c j i", i=4),
-                     raw[:, :, c : c + step].rearrange("p j (c i) -> p c j i", i=4))
+                copy(
+                    grouped[:, c : c + step, :].rearrange("p (c i) j -> p c j i", i=LINE),
+                    raw[:, :, c : c + step].rearrange("p j (c i) -> p c j i", i=LINE),
+                )
             nc.vector.quantize_mx(codes.bitcast(FP8X4), scales, grouped[:].rearrange("p c j -> p (c j)"))
             return grouped
 
         on_vector, on_scalar = nc.vector.tensor_copy, nc.scalar.copy
-        quantise("w2_bf01", w2_first[:], on_scalar, HALF, w2_codes[:, :HALF], w2_scales[:, :HALF], "w2_bf01")
-        quantise("w1_bf01", w1_raw[:, :, :HALF], on_vector, P, w1_codes[:, :HALF], w1_scales[:, :HALF], "w1_bf01")
-        quantise("w2_bf2", w2_second[:, :, :P], on_vector, P, w2_codes[:, HALF : HALF + P], w2_scales[:, HALF : HALF + P], "w2_bf2")
-        last = quantise("w1_bf23", w1_raw[:, :, HALF:], on_scalar, HALF, w1_codes[:, HALF:], w1_scales[:, HALF:], "slot_sq3")
-        quantise("w2_bf3", w2_second[:, :, P:], on_scalar, P, w2_codes[:, HALF + P :], w2_scales[:, HALF + P :], "slot_sq2")
+        first, second = slice(0, HALF), slice(HALF, ROWS)
+        third, fourth = slice(HALF, HALF + P), slice(HALF + P, ROWS)
+        quantise("w2_g01", w2_first[:], on_scalar, HALF, w2_codes[:, first], w2_scales[:, first], "w2_g01")
+        quantise("w1_g01", w1_raw[:, :, first], on_vector, P, w1_codes[:, first], w1_scales[:, first], "w1_g01")
+        quantise("w2_g2", w2_second[:, :, :P], on_vector, P, w2_codes[:, third], w2_scales[:, third], "w2_g2")
+        w1_g23 = quantise(
+            "w1_g23", w1_raw[:, :, second], on_scalar, HALF, w1_codes[:, second], w1_scales[:, second], "after_root3"
+        )
+        quantise("w2_g3", w2_second[:, :, P:], on_scalar, P, w2_codes[:, fourth], w2_scales[:, fourth], "after_root2")
+
         warm_exp = keep.tile([P, 1], F32, name="warm_exp")
-        nc.scalar.activation(warm_exp[:], last[:, 0, 0:1], ACT.Exp, scale=0.0, bias=inv_win[PACK - 1][:, 0:1])
+        nc.scalar.activation(warm_exp[:], w1_g23[:, 0, 0:1], ACT.Exp, scale=0.0, bias=inverse[PACK - 1][:, 0:1])
 
         for t in range(PACK):
             cols = slice(t * P, (t + 1) * P)
-            nc.tensor.matmul_mx(h_bank[t][:], lhsT=w2_codes[:, cols].bitcast(FP8X4), lhsT_scale=w2_scales[:, cols],
-                                rhs=x2_codes[:].bitcast(FP8X4), rhs_scale=x2_scales, start=True, stop=False)
-            nc.tensor.matmul_mx(h_bank[t][:], lhsT=w1_codes[:, cols].bitcast(FP8X4), lhsT_scale=w1_scales[:, cols],
-                                rhs=z_codes[:].bitcast(FP8X4), rhs_scale=z_scales[:], start=False, stop=True)
+            nc.tensor.matmul_mx(
+                h_bank[t][:],
+                lhsT=w2_codes[:, cols].bitcast(FP8X4),
+                lhsT_scale=w2_scales[:, cols],
+                rhs=x2_codes[:].bitcast(FP8X4),
+                rhs_scale=x2_scales,
+                start=True,
+                stop=False,
+            )
+            nc.tensor.matmul_mx(
+                h_bank[t][:],
+                lhsT=w1_codes[:, cols].bitcast(FP8X4),
+                lhsT_scale=w1_scales[:, cols],
+                rhs=z_codes[:].bitcast(FP8X4),
+                rhs_scale=z_scales[:],
+                start=False,
+                stop=True,
+            )
 
+        size_and_h = [keep.tile([P, 2 * PICKS], F32, name=f"size_and_h{t}") for t in range(PACK)]
         for t in range(PACK):
-            size_win = keep.tile([P, 2 * S], F32, name=f"size_win{t}")
-            gate = keep.tile([P, S], F32, name=f"gate{t}")
-            h_diff = keep.tile([P, S], F32, name=f"h_diff{t}")
-            result = keep.tile([P, S], F32, name=f"result{t}")
-            if t < 2:
-                nc.vector.tensor_scalar(neg_win[t][:, :S], h_bank[t][:], -1.0, None, ALU.mult)
+            if t < PACK - 1:
+                nc.vector.tensor_scalar(negated[t][:, :PICKS], h_bank[t][:], -1.0, None, ALU.mult)
             else:
-                nc.scalar.activation(neg_win[t][:, :S], h_bank[t][:], ACT.Copy, scale=-1.0)
-            nc.scalar.activation(size_win[:, :S], h_bank[t][:], ACT.Abs)
-            nc.vector.tensor_scalar(size_win[:, S:], neg_win[t][:, :S], -1.0, None, ALU.mult)
-            nc.scalar.activation(gate[:], size_win[:].indirect(n3_list[:]), ACT.Exp, scale=neg_rate[:, t : t + 1])
-            nc.vector.tensor_tensor(h_diff[:], neg_win[t][:].indirect(n4_list[:]), size_win[:, S:], ALU.add)
-            nc.vector.tensor_tensor(result[:], h_diff[:], gate[:], ALU.mult)
+                nc.scalar.activation(negated[t][:, :PICKS], h_bank[t][:], ACT.Copy, scale=-1.0)
+            nc.scalar.activation(size_and_h[t][:, :PICKS], h_bank[t][:], ACT.Abs)
+            nc.vector.tensor_scalar(size_and_h[t][:, PICKS:], negated[t][:, :PICKS], -1.0, None, ALU.mult)
+        for t in range(PACK):
+            ea = keep.tile([P, PICKS], F32, name=f"ea{t}")
+            h_diff = keep.tile([P, PICKS], F32, name=f"h_diff{t}")
+            result = keep.tile([P, PICKS], F32, name=f"result{t}")
+            nc.scalar.activation(ea[:], size_and_h[t][:].indirect(n3_list[:]), ACT.Exp, scale=neg_rate[:, t : t + 1])
+            nc.vector.tensor_tensor(h_diff[:], negated[t][:].indirect(n4_list[:]), size_and_h[t][:, PICKS:], ALU.add)
+            nc.vector.tensor_tensor(result[:], h_diff[:], ea[:], ALU.mult)
             nc.sync.dma_start(out[t * P : (t + 1) * P, :], result[:])

from contextlib import ExitStack

import concourse.mybir as mybir

F32 = mybir.dt.float32
BF16 = mybir.dt.bfloat16
I32 = mybir.dt.int32
U32 = mybir.dt.uint32
U16 = mybir.dt.uint16
U8 = mybir.dt.uint8
FP8X4 = mybir.dt.float8_e4m3fn_x4
ALU = mybir.AluOpType
ACT = mybir.ActivationFunctionType

P = 128
PACK = 4
TABLE = 2048
PICKS = 256
ROWS = 512
HALF = ROWS // 2
GROUP = 16
BLOCK = 8
QUADRANT = 32
LINE = 4
SPARE = 16
FLOPS = 3 * 2 * ROWS * ROWS * PICKS


def tile_picked_kmixhopnela_none_p_kernel(
    tc, x_words, x_scales, d_words, d_scales, gn, w1, w2, tau, offs, k1, n1, n2, two, n3, n4, out
):
    nc = tc.nc
    with ExitStack() as ctx:
        keep = ctx.enter_context(tc.tile_pool(name="keep", bufs=1))
        psum = ctx.enter_context(tc.psum_pool(name="psum", bufs=1))

        def load_list(name, src, entries):
            lst = keep.tile([P, entries // GROUP], U16, name=name)
            nc.sync.dma_start(lst[:], src)
            return lst

        d_byte_table = keep.tile([P, TABLE], U8, name="d_byte_table")
        x_byte_table = keep.tile([P, TABLE], U8, name="x_byte_table", tag="after_x_bytes")
        d_word_table = keep.tile([P, TABLE], U32, name="d_word_table", tag="after_d_words")
        x_word_table = keep.tile([P, TABLE], U32, name="x_word_table")

        nc.vector.memset(d_byte_table[:, : TABLE // 2].bitcast(I32), 0)
        nc.gpsimd.memset(d_byte_table[:, TABLE // 2 :].bitcast(I32), 0)
        nc.gpsimd.memset(x_byte_table[:].bitcast(I32), 0)
        nc.sync.dma_start(d_byte_table[0:P:BLOCK, :].bitcast(I32), d_scales[0].bitcast(I32))
        k1_list = load_list("k1_list", k1, ROWS)
        offs_list = load_list("offs_list", offs, PICKS)
        nc.sync.dma_start(d_word_table[:].bitcast(I32), d_words[0].rearrange("p c r -> p (c r)").bitcast(I32))
        nc.scalar.dma_start(x_byte_table[0:P:BLOCK, :].bitcast(I32), x_scales[0].bitcast(I32))
        two_list = load_list("two_list", two, PICKS)
        n1_list = load_list("n1_list", n1, PICKS)
        n2_list = load_list("n2_list", n2, PICKS)
        n3_list = load_list("n3_list", n3, PICKS)
        nc.sync.dma_start(x_word_table[:].bitcast(I32), x_words[0].rearrange("p c r -> p (c r)").bitcast(I32))
        w2_rows = w2.rearrange("(p j) c -> p j c", j=PACK)
        w2_first = keep.tile([P, PACK, HALF], F32, name="w2_first")
        nc.sync.dma_start(w2_first[:], w2_rows[:, :, :HALF])
        n4_list = load_list("n4_list", n4, PICKS)
        gain = keep.tile([P, PACK], F32, name="gain")
        nc.scalar.dma_start(gain[:], gn.rearrange("(p t) o -> p (t o)", t=PACK))

        negated = [keep.tile([P, PICKS + SPARE], F32, name=f"negated{t}") for t in range(PACK)]
        inverse = [keep.tile([P, PICKS + SPARE], F32, name=f"inverse{t}") for t in range(PACK)]
        for window in negated + inverse:
            nc.gpsimd.memset(window[:, PICKS:], 0.0)

        d_bytes = keep.tile([P, ROWS], U8, name="d_bytes")
        x_bytes = keep.tile([P, 2 * PICKS], U8, name="x_bytes", tag="after_x_copy")
        picked_scales = keep.tile([P, ROWS + 2 * PICKS], U8, name="picked_scales", align_bytes=64)
        nc.vector.tensor_copy(d_bytes[:], d_byte_table[:].indirect(k1_list[:]))
        nc.vector.tensor_copy(x_bytes[:, :PICKS], x_byte_table[:].indirect(offs_list[:]))
        nc.vector.tensor_copy(x_bytes[:, PICKS:], x_byte_table[:].indirect(two_list[:]))
        nc.vector.tensor_copy(
            picked_scales[:, :ROWS].rearrange("p (t m) -> p t m", t=PACK),
            d_bytes[:].rearrange("p (m t) -> p t m", t=PACK),
        )
        nc.vector.tensor_copy(picked_scales[:, ROWS:].bitcast(I32), x_bytes[:].bitcast(I32))
        for r in range(1, QUADRANT // BLOCK):
            nc.sync.dma_start(
                picked_scales[r:P:QUADRANT, :].bitcast(I32),
                picked_scales[BLOCK * r : P : QUADRANT, :].bitcast(I32),
            )
        xq_scales = picked_scales[:, ROWS : ROWS + PICKS]
        x2_scales = picked_scales[:, ROWS + PICKS :]

        d_picked = keep.tile([P, ROWS], U32, name="d_picked", tag="after_x_bytes")
        key_codes = keep.tile([P, ROWS], U32, name="key_codes", align_bytes=64)
        nc.vector.tensor_copy(d_picked[:], d_word_table[:].indirect(k1_list[:]))
        nc.vector.tensor_copy(
            key_codes[:].rearrange("p (t b i) -> p b t i", t=PACK, i=LINE),
            d_picked[:].rearrange("p (b i t) -> p b t i", t=PACK, i=LINE),
        )
        xq_codes = keep.tile([P, PICKS], U32, name="xq_codes", align_bytes=64)
        nc.vector.tensor_copy(xq_codes[:], x_word_table[:].indirect(offs_list[:]))

        w2_second = keep.tile([P, PACK, HALF], F32, name="w2_second", tag="after_x_copy")
        nc.sync.dma_start(w2_second[:], w2_rows[:, :, HALF:])
        w1_raw = keep.tile([P, PACK, ROWS], F32, name="w1_raw", tag="after_d_words")
        nc.sync.dma_start(w1_raw[:], w1.rearrange("(p j) c -> p j c", j=PACK))
        rate = keep.tile([P, PACK], F32, name="rate", tag="after_x_bytes")
        with nc.allow_non_contiguous_dma(reason="tau of row 128 t + p goes to [p, t]"):
            nc.sync.dma_start(rate[:], tau.rearrange("(t p) o -> p (t o)", p=P))

        neg_gain = keep.tile([P, PACK], F32, name="neg_gain")
        safe_gain = keep.tile([P, PACK], F32, name="safe_gain")
        inv_gain = keep.tile([P, PACK], F32, name="inv_gain")
        neg_rate = keep.tile([P, PACK], F32, name="neg_rate")
        nc.vector.tensor_scalar(neg_gain[:], gain[:], -1.0, None, ALU.mult)
        nc.vector.scalar_tensor_tensor(safe_gain[:], gain[:], 0.0, gain[:], ALU.is_equal, ALU.add)
        nc.vector.reciprocal(inv_gain[:], safe_gain[:])
        nc.gpsimd.tensor_scalar(neg_rate[:], rate[:], -1.0, 0.0, ALU.mult, ALU.add)
        eight = keep.tile([P, 1], F32, name="eight")
        nc.gpsimd.memset(eight[:], 8.0)

        warm_root = keep.tile([P, 1], F32, name="warm_root")
        nc.scalar.activation(warm_root[:], eight[:], ACT.Abs_reciprocal_sqrt)

        s_bank = [psum.tile([P, PICKS], F32, name=f"s_bank{t}") for t in range(PACK)]
        h_bank = [psum.tile([P, PICKS], F32, name=f"h_bank{t}") for t in range(PACK)]
        scored = [keep.tile([P, PICKS], F32, name=f"scored{t}") for t in range(PACK)]
        diff = [keep.tile([P, PICKS], F32, name=f"diff{t}") for t in range(PACK)]
        diff_size = [keep.tile([P, PICKS], F32, name=f"diff_size{t}") for t in range(PACK)]
        squared = [
            keep.tile([P, PICKS], F32, name=f"squared{t}", tag=f"after_root{t}", align_bytes=64) for t in range(PACK)
        ]
        z_rows = keep.tile([P, PACK, PICKS], F32, name="z_rows")
        for t in range(PACK):
            cols = slice(t * P, (t + 1) * P)
            nc.tensor.matmul_mx(
                s_bank[t][:],
                lhsT=key_codes[:, cols].bitcast(FP8X4),
                lhsT_scale=picked_scales[:, cols],
                rhs=xq_codes[:].bitcast(FP8X4),
                rhs_scale=xq_scales,
                start=True,
                stop=True,
            )
        for t in range(PACK):
            nc.scalar.activation(negated[t][:, :PICKS], s_bank[t][:], ACT.Copy, scale=neg_gain[:, t : t + 1])
            nc.scalar.activation(scored[t][:], s_bank[t][:], ACT.Copy, scale=gain[:, t : t + 1])
            nc.vector.tensor_tensor(diff[t][:], negated[t][:].indirect(n1_list[:]), scored[t][:], ALU.add)
        for t in range(PACK):
            nc.scalar.activation(diff_size[t][:], diff[t][:], ACT.Abs, scale=inv_gain[:, t : t + 1])
            nc.scalar.activation(squared[t][:], diff_size[t][:], ACT.Square, bias=eight[:])
            nc.scalar.activation(inverse[t][:, :PICKS], squared[t][:], ACT.Abs_reciprocal_sqrt)
            nc.vector.tensor_tensor(z_rows[:, t, :], inverse[t][:].indirect(n2_list[:]), diff[t][:], ALU.mult)

        z_grouped = keep.tile([P, PICKS, PACK], BF16, name="z_grouped", align_bytes=64)
        z_codes = keep.tile([P, PICKS], U32, name="z_codes", align_bytes=64)
        z_scales = keep.tile([P, PICKS], U8, name="z_scales", align_bytes=64)
        nc.vector.tensor_copy(
            z_grouped[:].rearrange("p (c i) t -> p c t i", i=LINE),
            z_rows[:].rearrange("p t (c i) -> p c t i", i=LINE),
        )
        nc.vector.quantize_mx(z_codes[:].bitcast(FP8X4), z_scales[:], z_grouped[:].rearrange("p c t -> p (c t)"))

        x2_codes = keep.tile([P, PICKS], U32, name="x2_codes", align_bytes=64)
        nc.vector.tensor_copy(x2_codes[:], x_word_table[:].indirect(two_list[:]))

        w1_codes = keep.tile([P, ROWS], U32, name="w1_codes", align_bytes=64)
        w2_codes = keep.tile([P, ROWS], U32, name="w2_codes", align_bytes=64)
        w1_scales = keep.tile([P, ROWS], U8, name="w1_scales", align_bytes=64)
        w2_scales = keep.tile([P, ROWS], U8, name="w2_scales", align_bytes=64)

        def quantise(name, raw, copy, step, codes, scales, tag):
            width = raw.shape[2]
            grouped = keep.tile([P, width, PACK], BF16, name=name, tag=tag, align_bytes=64)
            for c in range(0, width, step):
                copy(
                    grouped[:, c : c + step, :].rearrange("p (c i) j -> p c j i", i=LINE),
                    raw[:, :, c : c + step].rearrange("p j (c i) -> p c j i", i=LINE),
                )
            nc.vector.quantize_mx(codes.bitcast(FP8X4), scales, grouped[:].rearrange("p c j -> p (c j)"))
            return grouped

        on_vector, on_scalar = nc.vector.tensor_copy, nc.scalar.copy
        first, second = slice(0, HALF), slice(HALF, ROWS)
        third, fourth = slice(HALF, HALF + P), slice(HALF + P, ROWS)
        quantise("w2_g01", w2_first[:], on_scalar, HALF, w2_codes[:, first], w2_scales[:, first], "w2_g01")
        quantise("w1_g01", w1_raw[:, :, first], on_vector, P, w1_codes[:, first], w1_scales[:, first], "w1_g01")
        quantise("w2_g2", w2_second[:, :, :P], on_vector, P, w2_codes[:, third], w2_scales[:, third], "w2_g2")
        w1_g23 = quantise(
            "w1_g23", w1_raw[:, :, second], on_scalar, HALF, w1_codes[:, second], w1_scales[:, second], "after_root3"
        )
        quantise("w2_g3", w2_second[:, :, P:], on_scalar, P, w2_codes[:, fourth], w2_scales[:, fourth], "after_root2")

        warm_exp = keep.tile([P, 1], F32, name="warm_exp")
        nc.scalar.activation(warm_exp[:], w1_g23[:, 0, 0:1], ACT.Exp, scale=0.0, bias=inverse[PACK - 1][:, 0:1])

        for t in range(PACK):
            cols = slice(t * P, (t + 1) * P)
            nc.tensor.matmul_mx(
                h_bank[t][:],
                lhsT=w2_codes[:, cols].bitcast(FP8X4),
                lhsT_scale=w2_scales[:, cols],
                rhs=x2_codes[:].bitcast(FP8X4),
                rhs_scale=x2_scales,
                start=True,
                stop=False,
            )
            nc.tensor.matmul_mx(
                h_bank[t][:],
                lhsT=w1_codes[:, cols].bitcast(FP8X4),
                lhsT_scale=w1_scales[:, cols],
                rhs=z_codes[:].bitcast(FP8X4),
                rhs_scale=z_scales[:],
                start=False,
                stop=True,
            )

        size_and_h = [keep.tile([P, 2 * PICKS], F32, name=f"size_and_h{t}") for t in range(PACK)]
        for t in range(PACK):
            if t < PACK - 1:
                nc.vector.tensor_scalar(negated[t][:, :PICKS], h_bank[t][:], -1.0, None, ALU.mult)
            else:
                nc.scalar.activation(negated[t][:, :PICKS], h_bank[t][:], ACT.Copy, scale=-1.0)
            nc.scalar.activation(size_and_h[t][:, :PICKS], h_bank[t][:], ACT.Abs)
            nc.vector.tensor_scalar(size_and_h[t][:, PICKS:], negated[t][:, :PICKS], -1.0, None, ALU.mult)
        for t in range(PACK):
            ea = keep.tile([P, PICKS], F32, name=f"ea{t}")
            h_diff = keep.tile([P, PICKS], F32, name=f"h_diff{t}")
            result = keep.tile([P, PICKS], F32, name=f"result{t}")
            nc.scalar.activation(ea[:], size_and_h[t][:].indirect(n3_list[:]), ACT.Exp, scale=neg_rate[:, t : t + 1])
            nc.vector.tensor_tensor(h_diff[:], negated[t][:].indirect(n4_list[:]), size_and_h[t][:, PICKS:], ALU.add)
            nc.vector.tensor_tensor(result[:], h_diff[:], ea[:], ALU.mult)
            nc.sync.dma_start(out[t * P : (t + 1) * P, :], result[:])
